import numpy as np
import ml_dtypes


def mxq(x, axis, fmt="e4m3"):
    dtype, down = {"e4m3": (ml_dtypes.float8_e4m3fn, 7), "e5m2": (ml_dtypes.float8_e5m2, 14)}[fmt]
    v = np.moveaxis(np.asarray(x, np.float32).astype(ml_dtypes.bfloat16).astype(np.float64), axis, -1)
    blocks = v.reshape(v.shape[:-1] + (-1, 32))
    amax = np.abs(blocks).max(-1, keepdims=True)
    byte = np.maximum(np.where(amax > 0, np.frexp(amax)[1] - 1 + 127, 0) - down, 1)
    scale = np.exp2(byte - 127.0)
    codes = (blocks / scale).astype(np.float32).astype(dtype).astype(np.float64)
    return np.moveaxis((codes * scale).reshape(v.shape), -1, axis)


WIDE = False


def mx_kscale(k):
    if not WIDE:
        return np.ones(k)
    levels = np.array([30, -30])
    if k % 512:
        return np.exp2(np.random.permutation(np.resize(levels, k // 32))).repeat(32)
    a = np.empty((k // 512, 16))
    for p in range(k // 512):
        a[p, :8] = np.random.permutation(np.resize(levels, 8))
        for g in range(8):
            far = levels[np.abs(levels - a[p, g]) >= 10]
            a[p, g + 8] = far[np.random.randint(len(far))]
    return np.exp2(a.ravel()).repeat(32)


def f64(x):
    return np.asarray(x).astype(np.float64)


def striped(idx):
    return np.tile(np.asarray(idx).reshape(-1, 16).T, (8, 1)).astype(np.uint16)


def unstriped(offs):
    return offs[:16].T.reshape(-1).astype(np.int64)


def striped8(idx):
    return np.asarray(idx).reshape(8, -1, 16).transpose(0, 2, 1).reshape(128, -1).astype(np.uint16)


def unstriped8(offs):
    return offs.reshape(8, 16, -1).transpose(0, 2, 1).reshape(8, -1).astype(np.int64)


def pick8(x, idx, run):
    r = np.arange(len(x))
    return x[r[:, None], idx[r % (8 * run) // run]]


E2M1 = np.array([0.0, 0.5, 1.0, 1.5, 2.0, 3.0, 4.0, 6.0, -0.0, -0.5, -1.0, -1.5, -2.0, -3.0, -4.0, -6.0])


def pack_weight(w, fmt):
    k, n = w.shape
    w = f64(np.asarray(w, np.float32).astype(ml_dtypes.bfloat16)).reshape(k // 32, 32, n)
    amax = np.abs(w).max(1)
    if fmt in ("e4m3", "e5m2"):
        byte = np.frexp(amax)[1] - 1 + 127 - (7 if fmt == "e4m3" else 14)
    else:
        mant, ex = np.frexp(amax / 6.0)
        byte = np.where(mant > 0.5, ex, ex - 1) + 127
    byte = np.clip(np.where(amax > 0, byte, 1), 1, 254)
    scaled = (w * np.exp2(127.0 - byte)[:, None, :]).reshape(k, n).astype(np.float32)
    by_word = np.ascontiguousarray(scaled.reshape(k // 512, 128, 4, n).transpose(0, 1, 3, 2))
    if fmt in ("e4m3", "e5m2"):
        words = by_word.astype(ml_dtypes.float8_e4m3fn if fmt == "e4m3" else ml_dtypes.float8_e5m2).view(np.uint8)
    else:
        c = by_word.astype(ml_dtypes.float4_e2m1fn).view(np.uint8) & 0xF
        words = (c[..., 0::2] | (c[..., 1::2] << 4)).reshape(k // 512, 128, 2 * n)
    return np.ascontiguousarray(words), np.ascontiguousarray(byte.astype(np.uint8).reshape(k // 512, 16, n))


def unpack_weight(words, scales, fmt):
    g, _, n = scales.shape
    words = np.ascontiguousarray(words).reshape(g, 128, n, -1)
    if fmt in ("e4m3", "e5m2"):
        vals = words.view(ml_dtypes.float8_e4m3fn if fmt == "e4m3" else ml_dtypes.float8_e5m2).astype(np.float64)
    else:
        nib = np.empty((g, 128, n, 4), np.uint8)
        nib[..., 0::2] = words & 0xF
        nib[..., 1::2] = words >> 4
        vals = E2M1[nib]
    vals = vals * np.repeat(np.exp2(scales.astype(np.float64) - 127.0), 8, axis=1)[..., None]
    return vals.transpose(0, 1, 3, 2).reshape(g * 512, n)


K, T, J, R, N, E = 512, 2048, 256, 512, 256, 512


def setup_inputs():
    n = np.random.standard_normal
    idx = np.random.permutation(T)[:J]
    idx2 = np.random.permutation(T)[:J]
    idx3 = np.stack([np.random.permutation(E)[:J] for _ in range(8)])
    idx4 = np.stack([np.random.permutation(E)[:J] for _ in range(8)])
    fk = mx_kscale(K)
    fr = mx_kscale(R)
    xtp = pack_weight(n((K, T)) / fk[:, None], "e2m1")
    wp = pack_weight(n((K, R)) * 1 / np.sqrt(K) * fk[:, None] * fr, "e5m2")
    w2p = pack_weight(n((K, R)) * 1 / np.sqrt(K) * fk[:, None] * fr, "e4m3")
    wbp = pack_weight(n((R, N)) * 1 / np.sqrt(R) / fr[:, None], "e4m3")
    wcp = pack_weight(n((R, N)) * 1 / np.sqrt(R) / fr[:, None], "e2m1")
    return {
        "xt_words": xtp[0],
        "xt_scales": xtp[1],
        "w_words": wp[0],
        "w_scales": wp[1],
        "w2_words": w2p[0],
        "w2_scales": w2p[1],
        "wb_words": wbp[0],
        "wb_scales": wbp[1],
        "wc_words": wcp[0],
        "wc_scales": wcp[1],
        "offs": striped(idx),
        "offs2": striped(idx2),
        "offs3": striped8(idx3),
        "offs4": striped8(idx4),
    }


def reference(xt_words, xt_scales, w_words, w_scales, w2_words, w2_scales, wb_words, wb_scales, wc_words, wc_scales, offs, offs2, offs3, offs4):
    idx = unstriped(offs)
    idx2 = unstriped(offs2)
    idx3 = unstriped8(offs3)
    idx4 = unstriped8(offs4)
    xtu = unpack_weight(xt_words, xt_scales, "e2m1")
    wu = unpack_weight(w_words, w_scales, "e5m2")
    w2u = unpack_weight(w2_words, w2_scales, "e4m3")
    wbu = unpack_weight(wb_words, wb_scales, "e4m3")
    wcu = unpack_weight(wc_words, wc_scales, "e2m1")
    xtidxg = xtu[:, idx]
    a = wu.T @ xtidxg
    xtidx2g = xtu[:, idx2]
    b = w2u.T @ xtidx2g
    hid = np.maximum(a, b)
    hidq = mxq(hid, 0, "e5m2")
    p = wbu.T @ hidq
    q = wcu.T @ hidq
    pw = np.zeros((N, E))
    pw[np.arange(N)[:, None], idx3[np.arange(N) % 128 // 16]] = p
    pv = np.zeros((N, E))
    pv[np.arange(N)[:, None], idx4[np.arange(N) % 128 // 16]] = q
    y = np.maximum(pw, pv)
    return y

@@ -1,0 +1,192 @@
+from contextlib import ExitStack
+
+import concourse.mybir as mybir
+
+K, T, J, R, N, E = 512, 2048, 256, 512, 256, 512
+FLOPS = 2 * (2 * K * R * J + 2 * R * N * J)
+
+F32 = mybir.dt.float32
+BF16 = mybir.dt.bfloat16
+I32 = mybir.dt.int32
+U32 = mybir.dt.uint32
+U16 = mybir.dt.uint16
+U8 = mybir.dt.uint8
+E4M3 = mybir.dt.float8_e4m3fn_x4
+E5M2 = mybir.dt.float8_e5m2_x4
+E2M1 = mybir.dt.float4_e2m1fn_x4
+COPY = mybir.ActivationFunctionType.Copy
+MAX = mybir.AluOpType.max
+
+P = 128
+PACK = 4
+HALF = J // 2
+LIST_COLS = J // 16
+
+
+def tile_list_outcomeownpages_ahead_kernel(
+    tc, xt_words, xt_scales, w_words, w_scales, w2_words, w2_scales, wb_words, wb_scales,
+    wc_words, wc_scales, offs, offs2, offs3, offs4, out,
+):
+    nc = tc.nc
+    with ExitStack() as ctx:
+        sb = ctx.enter_context(tc.tile_pool(name="sb", bufs=1))
+        ps = ctx.enter_context(tc.psum_pool(name="ps", bufs=1))
+
+        def tile(name, shape, dtype):
+            return sb.tile(shape, dtype, name=name, align_bytes=64)
+
+        lists = [tile("list%d" % i, [P, LIST_COLS], U16) for i in range(4)]
+        x_words = tile("x_words", [P, T], U16)
+        x_plane = tile("x_plane", [P, T], U8)
+        w_raw = [tile("w_raw%d" % i, [P, R], U32) for i in range(2)]
+        w_dealt = [tile("w_dealt%d" % i, [P, R], U32) for i in range(2)]
+        ws_raw = [tile("ws_raw%d" % i, [P, 4 * R], U8) for i in range(2)]
+        ws_dealt = [tile("ws_dealt%d" % i, [P, R], U8) for i in range(2)]
+        wb_sb = tile("wb_sb", [P, N], U32)
+        wc_sb = tile("wc_sb", [P, 2 * N], U8)
+        os_raw = [tile("os_raw%d" % i, [P, N], U8) for i in range(2)]
+        pages = [[tile("page%d" % s, [P, E], F32)] for s in range(2)]
+
+        for raw, width in [(ws_raw[0], R), (ws_raw[1], R), (x_plane, T), (os_raw[0], N), (os_raw[1], N)]:
+            nc.vector.memset(raw[:, 0:width].bitcast(I32), 0)
+        for s in range(2):
+            nc.vector.memset(pages[s][0][:], 0.0)
+
+        def load_words(queue, dst, src):
+            queue.dma_start(dst[:].bitcast(I32), src.bitcast(I32))
+
+        def load_scale_rows(queue, raw, scales):
+            rows = scales[0].bitcast(I32).rearrange("(q r) w -> r q w", q=4)
+            queue.dma_start(raw[0:4, :].bitcast(I32).rearrange("p (q w) -> p q w", q=4), rows)
+
+        def spread_scale_rows(raw):
+            words = raw[:].bitcast(I32)
+            width = words.shape[1] // 4
+            for q in range(1, 4):
+                nc.vector.tensor_copy(words[32 * q : 32 * q + 4, 0:width], words[0:4, q * width : (q + 1) * width])
+
+        def load_plane(plane, scales):
+            for q in range(4):
+                nc.sync.dma_start(
+                    plane[32 * q : 32 * q + 4, :].bitcast(I32),
+                    scales[0, 4 * q : 4 * q + 4, :].bitcast(I32),
+                )
+
+        nc.sync.dma_start(lists[0][:], offs)
+        load_scale_rows(nc.sync, ws_raw[0], w_scales)
+        load_scale_rows(nc.sync, ws_raw[1], w2_scales)
+        load_words(nc.sync, x_words, xt_words[0])
+        load_plane(x_plane, xt_scales)
+        load_words(nc.sync, w_raw[0], w_words[0].rearrange("p c t -> p (c t)"))
+        nc.sync.dma_start(lists[1][:], offs2)
+        load_words(nc.sync, w_raw[1], w2_words[0].rearrange("p c t -> p (c t)"))
+        load_words(nc.sync, wb_sb, wb_words[0].rearrange("p c t -> p (c t)"))
+        load_plane(os_raw[0], wb_scales)
+        nc.sync.dma_start(lists[2][:], offs3)
+        load_words(nc.sync, wc_sb, wc_words[0])
+        load_plane(os_raw[1], wc_scales)
+        nc.sync.dma_start(lists[3][:], offs4)
+
+        picked_words = [tile("picked_words%d" % i, [P, J], U16) for i in range(2)]
+        picked_plane = [tile("picked_plane%d" % i, [P, J], U8) for i in range(2)]
+        for i in range(2):
+            nc.scalar.copy(
+                w_dealt[i][:].rearrange("p (t c u) -> p c t u", t=PACK, u=4),
+                w_raw[i][:].rearrange("p (c u t) -> p c t u", t=PACK, u=4),
+            )
+            spread_scale_rows(ws_raw[i])
+        for i in range(2):
+            nc.vector.tensor_copy(
+                ws_dealt[i][:].rearrange("p (t m) -> p t m", t=PACK),
+                ws_raw[i][:, 0:R].rearrange("p (m t) -> p t m", t=PACK),
+            )
+        for i in range(2):
+            nc.vector.tensor_copy(picked_words[i][:], x_words[:].indirect(lists[i][:]))
+            nc.vector.tensor_copy(picked_plane[i][:], x_plane[:].indirect(lists[i][:]))
+
+        def first_stage(i, h, fmt, bank):
+            acc = ps.tile([P, PACK, HALF], F32, name=bank)
+            cols = slice(h * HALF, (h + 1) * HALF)
+            for t in range(PACK):
+                rows = slice(t * P, (t + 1) * P)
+                nc.tensor.matmul_mx(
+                    acc[:, t, :],
+                    lhsT=w_dealt[i][:, rows].bitcast(fmt),
+                    lhsT_scale=ws_dealt[i][:, rows],
+                    rhs=picked_words[i][:, cols].bitcast(E2M1),
+                    rhs_scale=picked_plane[i][:, cols],
+                    start=True,
+                    stop=True,
+                )
+            return acc
+
+        a_sb = []
+        b_acc = []
+        for h in range(2):
+            a_acc = first_stage(0, h, E5M2, "a_bank%d" % h)
+            a_half = tile("a_half%d" % h, [P, HALF, PACK], F32)
+            nc.scalar.activation(a_half[:], a_acc[:].rearrange("p t j -> p j t"), COPY)
+            a_sb.append(a_half)
+            b_acc.append(first_stage(1, h, E4M3, "b_bank%d" % h))
+        for s, slot in enumerate(["x_words", "x_plane"]):
+            page = tile(slot, [P, E], F32)
+            nc.gpsimd.memset(page[:], 0.0)
+            pages[s].append(page)
+
+        codes = tile("codes", [P, J], U32)
+        plane = tile("plane", [P, J], U8)
+
+        def quantise(h):
+            hid = tile("hid%d" % h, [P, HALF, PACK], BF16)
+            nc.vector.tensor_tensor(hid[:], b_acc[h][:].rearrange("p t j -> p j t"), a_sb[h][:], MAX)
+            cols = slice(h * HALF, (h + 1) * HALF)
+            nc.vector.quantize_mx(
+                codes[:, cols].bitcast(E5M2), plane[:, cols], hid[:].rearrange("p j t -> p (j t)")
+            )
+
+        def second_stage(acc, s, g, cols):
+            rows = slice(g * P, (g + 1) * P)
+            if s == 0:
+                weights = wb_sb[:, rows].bitcast(E4M3)
+            else:
+                weights = wc_sb[:, 2 * g * P : 2 * (g + 1) * P].bitcast(E2M1)
+            nc.tensor.matmul_mx(
+                acc, lhsT=weights, lhsT_scale=os_raw[s][:, rows],
+                rhs=codes[:, cols].bitcast(E5M2), rhs_scale=plane[:, cols], start=True, stop=True,
+            )
+
+        def scatter(s, g, cols, values):
+            entries = slice(cols.start // 16, cols.stop // 16)
+            nc.scalar.activation(pages[s][g][:].indirect(lists[2 + s][:, entries]), values, COPY)
+
+        def finish(g, parts):
+            width = E // parts
+            for c in range(parts):
+                cols = slice(c * width, (c + 1) * width)
+                y = tile("y%d%d" % (g, c), [P, width], F32)
+                nc.vector.tensor_tensor(y[:], pages[0][g][:, cols], pages[1][g][:, cols], MAX)
+                queue = nc.scalar if c == 1 else nc.sync
+                queue.dma_start(out[g * P : (g + 1) * P, cols], y[:])
+
+        first, second, whole = slice(0, HALF), slice(HALF, J), slice(0, J)
+        quantise(0)
+        for s in range(2):
+            acc = ps.tile([P, HALF], F32, name="early%d" % s)
+            second_stage(acc[:], s, 0, first)
+            outcome = tile("early_outcome%d" % s, [P, HALF], F32)
+            if s == 0:
+                nc.scalar.copy(outcome[:], acc[:])
+            else:
+                nc.vector.tensor_copy(outcome[:], acc[:])
+            scatter(s, 0, first, outcome[:])
+        quantise(1)
+        for g, cols in [(0, second), (1, whole)]:
+            width = cols.stop - cols.start
+            acc = ps.tile([P, 2, width], F32, name="late%d" % g)
+            for s in range(2):
+                second_stage(acc[:, s, :], s, g, cols)
+            outcome = tile("late_outcome%d" % g, [P, 2, width], F32)
+            nc.vector.tensor_copy(outcome[:], acc[:])
+            for s in range(2):
+                scatter(s, g, cols, outcome[:, s, :])
+            finish(g, g + 1)

@@ -96,7 +96,7 @@ def tile_list_outcomeownpages_ahead_kernel(
             )
             spread_scale_rows(ws_raw[i])
         for i in range(2):
-            nc.vector.tensor_copy(
+            nc.gpsimd.tensor_copy(
                 ws_dealt[i][:].rearrange("p (t m) -> p t m", t=PACK),
                 ws_raw[i][:, 0:R].rearrange("p (m t) -> p t m", t=PACK),
             )

from contextlib import ExitStack

import concourse.mybir as mybir

K, T, J, R, N, E = 512, 2048, 256, 512, 256, 512
FLOPS = 2 * (2 * K * R * J + 2 * R * N * J)

F32 = mybir.dt.float32
BF16 = mybir.dt.bfloat16
I32 = mybir.dt.int32
U32 = mybir.dt.uint32
U16 = mybir.dt.uint16
U8 = mybir.dt.uint8
E4M3 = mybir.dt.float8_e4m3fn_x4
E5M2 = mybir.dt.float8_e5m2_x4
E2M1 = mybir.dt.float4_e2m1fn_x4
COPY = mybir.ActivationFunctionType.Copy
MAX = mybir.AluOpType.max

P = 128
PACK = 4
HALF = J // 2
LIST_COLS = J // 16


def tile_list_outcomeownpages_ahead_kernel(
    tc, xt_words, xt_scales, w_words, w_scales, w2_words, w2_scales, wb_words, wb_scales,
    wc_words, wc_scales, offs, offs2, offs3, offs4, out,
):
    nc = tc.nc
    with ExitStack() as ctx:
        sb = ctx.enter_context(tc.tile_pool(name="sb", bufs=1))
        ps = ctx.enter_context(tc.psum_pool(name="ps", bufs=1))

        def tile(name, shape, dtype):
            return sb.tile(shape, dtype, name=name, align_bytes=64)

        lists = [tile("list%d" % i, [P, LIST_COLS], U16) for i in range(4)]
        x_words = tile("x_words", [P, T], U16)
        x_plane = tile("x_plane", [P, T], U8)
        w_raw = [tile("w_raw%d" % i, [P, R], U32) for i in range(2)]
        w_dealt = [tile("w_dealt%d" % i, [P, R], U32) for i in range(2)]
        ws_raw = [tile("ws_raw%d" % i, [P, 4 * R], U8) for i in range(2)]
        ws_dealt = [tile("ws_dealt%d" % i, [P, R], U8) for i in range(2)]
        wb_sb = tile("wb_sb", [P, N], U32)
        wc_sb = tile("wc_sb", [P, 2 * N], U8)
        os_raw = [tile("os_raw%d" % i, [P, N], U8) for i in range(2)]
        pages = [[tile("page%d" % s, [P, E], F32)] for s in range(2)]

        for raw, width in [(ws_raw[0], R), (ws_raw[1], R), (x_plane, T), (os_raw[0], N), (os_raw[1], N)]:
            nc.vector.memset(raw[:, 0:width].bitcast(I32), 0)
        for s in range(2):
            nc.vector.memset(pages[s][0][:], 0.0)

        def load_words(queue, dst, src):
            queue.dma_start(dst[:].bitcast(I32), src.bitcast(I32))

        def load_scale_rows(queue, raw, scales):
            rows = scales[0].bitcast(I32).rearrange("(q r) w -> r q w", q=4)
            queue.dma_start(raw[0:4, :].bitcast(I32).rearrange("p (q w) -> p q w", q=4), rows)

        def spread_scale_rows(raw):
            words = raw[:].bitcast(I32)
            width = words.shape[1] // 4
            for q in range(1, 4):
                nc.vector.tensor_copy(words[32 * q : 32 * q + 4, 0:width], words[0:4, q * width : (q + 1) * width])

        def load_plane(plane, scales):
            for q in range(4):
                nc.sync.dma_start(
                    plane[32 * q : 32 * q + 4, :].bitcast(I32),
                    scales[0, 4 * q : 4 * q + 4, :].bitcast(I32),
                )

        nc.sync.dma_start(lists[0][:], offs)
        load_scale_rows(nc.sync, ws_raw[0], w_scales)
        load_scale_rows(nc.sync, ws_raw[1], w2_scales)
        load_words(nc.sync, x_words, xt_words[0])
        load_plane(x_plane, xt_scales)
        load_words(nc.sync, w_raw[0], w_words[0].rearrange("p c t -> p (c t)"))
        nc.sync.dma_start(lists[1][:], offs2)
        load_words(nc.sync, w_raw[1], w2_words[0].rearrange("p c t -> p (c t)"))
        load_words(nc.sync, wb_sb, wb_words[0].rearrange("p c t -> p (c t)"))
        load_plane(os_raw[0], wb_scales)
        nc.sync.dma_start(lists[2][:], offs3)
        load_words(nc.sync, wc_sb, wc_words[0])
        load_plane(os_raw[1], wc_scales)
        nc.sync.dma_start(lists[3][:], offs4)

        picked_words = [tile("picked_words%d" % i, [P, J], U16) for i in range(2)]
        picked_plane = [tile("picked_plane%d" % i, [P, J], U8) for i in range(2)]
        for i in range(2):
            nc.scalar.copy(
                w_dealt[i][:].rearrange("p (t c u) -> p c t u", t=PACK, u=4),
                w_raw[i][:].rearrange("p (c u t) -> p c t u", t=PACK, u=4),
            )
            spread_scale_rows(ws_raw[i])
        for i in range(2):
            nc.gpsimd.tensor_copy(
                ws_dealt[i][:].rearrange("p (t m) -> p t m", t=PACK),
                ws_raw[i][:, 0:R].rearrange("p (m t) -> p t m", t=PACK),
            )
        for i in range(2):
            nc.vector.tensor_copy(picked_words[i][:], x_words[:].indirect(lists[i][:]))
            nc.vector.tensor_copy(picked_plane[i][:], x_plane[:].indirect(lists[i][:]))

        def first_stage(i, h, fmt, bank):
            acc = ps.tile([P, PACK, HALF], F32, name=bank)
            cols = slice(h * HALF, (h + 1) * HALF)
            for t in range(PACK):
                rows = slice(t * P, (t + 1) * P)
                nc.tensor.matmul_mx(
                    acc[:, t, :],
                    lhsT=w_dealt[i][:, rows].bitcast(fmt),
                    lhsT_scale=ws_dealt[i][:, rows],
                    rhs=picked_words[i][:, cols].bitcast(E2M1),
                    rhs_scale=picked_plane[i][:, cols],
                    start=True,
                    stop=True,
                )
            return acc

        a_sb = []
        b_acc = []
        for h in range(2):
            a_acc = first_stage(0, h, E5M2, "a_bank%d" % h)
            a_half = tile("a_half%d" % h, [P, HALF, PACK], F32)
            nc.scalar.activation(a_half[:], a_acc[:].rearrange("p t j -> p j t"), COPY)
            a_sb.append(a_half)
            b_acc.append(first_stage(1, h, E4M3, "b_bank%d" % h))
        for s, slot in enumerate(["x_words", "x_plane"]):
            page = tile(slot, [P, E], F32)
            nc.gpsimd.memset(page[:], 0.0)
            pages[s].append(page)

        codes = tile("codes", [P, J], U32)
        plane = tile("plane", [P, J], U8)

        def quantise(h):
            hid = tile("hid%d" % h, [P, HALF, PACK], BF16)
            nc.vector.tensor_tensor(hid[:], b_acc[h][:].rearrange("p t j -> p j t"), a_sb[h][:], MAX)
            cols = slice(h * HALF, (h + 1) * HALF)
            nc.vector.quantize_mx(
                codes[:, cols].bitcast(E5M2), plane[:, cols], hid[:].rearrange("p j t -> p (j t)")
            )

        def second_stage(acc, s, g, cols):
            rows = slice(g * P, (g + 1) * P)
            if s == 0:
                weights = wb_sb[:, rows].bitcast(E4M3)
            else:
                weights = wc_sb[:, 2 * g * P : 2 * (g + 1) * P].bitcast(E2M1)
            nc.tensor.matmul_mx(
                acc, lhsT=weights, lhsT_scale=os_raw[s][:, rows],
                rhs=codes[:, cols].bitcast(E5M2), rhs_scale=plane[:, cols], start=True, stop=True,
            )

        def scatter(s, g, cols, values):
            entries = slice(cols.start // 16, cols.stop // 16)
            nc.scalar.activation(pages[s][g][:].indirect(lists[2 + s][:, entries]), values, COPY)

        def finish(g, parts):
            width = E // parts
            for c in range(parts):
                cols = slice(c * width, (c + 1) * width)
                y = tile("y%d%d" % (g, c), [P, width], F32)
                nc.vector.tensor_tensor(y[:], pages[0][g][:, cols], pages[1][g][:, cols], MAX)
                queue = nc.scalar if c == 1 else nc.sync
                queue.dma_start(out[g * P : (g + 1) * P, cols], y[:])

        first, second, whole = slice(0, HALF), slice(HALF, J), slice(0, J)
        quantise(0)
        for s in range(2):
            acc = ps.tile([P, HALF], F32, name="early%d" % s)
            second_stage(acc[:], s, 0, first)
            outcome = tile("early_outcome%d" % s, [P, HALF], F32)
            if s == 0:
                nc.scalar.copy(outcome[:], acc[:])
            else:
                nc.vector.tensor_copy(outcome[:], acc[:])
            scatter(s, 0, first, outcome[:])
        quantise(1)
        for g, cols in [(0, second), (1, whole)]:
            width = cols.stop - cols.start
            acc = ps.tile([P, 2, width], F32, name="late%d" % g)
            for s in range(2):
                second_stage(acc[:, s, :], s, g, cols)
            outcome = tile("late_outcome%d" % g, [P, 2, width], F32)
            nc.vector.tensor_copy(outcome[:], acc[:])
            for s in range(2):
                scatter(s, g, cols, outcome[:, s, :])
            finish(g, g + 1)
